import numpy as np
import ml_dtypes


def mxq(x, axis, fmt="e4m3"):
    dtype, down = {"e4m3": (ml_dtypes.float8_e4m3fn, 7), "e5m2": (ml_dtypes.float8_e5m2, 14)}[fmt]
    v = np.moveaxis(np.asarray(x, np.float32).astype(ml_dtypes.bfloat16).astype(np.float64), axis, -1)
    blocks = v.reshape(v.shape[:-1] + (-1, 32))
    amax = np.abs(blocks).max(-1, keepdims=True)
    byte = np.maximum(np.where(amax > 0, np.frexp(amax)[1] - 1 + 127, 0) - down, 1)
    scale = np.exp2(byte - 127.0)
    codes = (blocks / scale).astype(np.float32).astype(dtype).astype(np.float64)
    return np.moveaxis((codes * scale).reshape(v.shape), -1, axis)


WIDE = False


def mx_kscale(k):
    if not WIDE:
        return np.ones(k)
    levels = np.array([10, -10, 5, -5, 0])
    if k % 512:
        return np.exp2(np.random.permutation(np.resize(levels, k // 32))).repeat(32)
    a = np.empty((k // 512, 16))
    for p in range(k // 512):
        a[p, :8] = np.random.permutation(np.resize(levels, 8))
        for g in range(8):
            far = levels[np.abs(levels - a[p, g]) >= 10]
            a[p, g + 8] = far[np.random.randint(len(far))]
    return np.exp2(a.ravel()).repeat(32)


def f64(x):
    return np.asarray(x).astype(np.float64)


def striped(idx):
    return np.tile(idx.reshape(-1, 16).T, (8, 1)).astype(np.uint16)


def unstriped(offs):
    return offs[:16].T.reshape(-1).astype(np.int64)


def striped8(idx):
    return np.concatenate([x.reshape(-1, 16).T for x in idx]).astype(np.uint16)


def runs(offs, k):
    lists = np.stack([offs[16 * r : 16 * r + 16].T.reshape(-1) for r in range(8)]).astype(np.int64)
    return lists[np.arange(k) % 512 // 64]


def pack_weight(w):
    k, n = w.shape
    w = f64(np.asarray(w, np.float32).astype(ml_dtypes.bfloat16)).reshape(k // 32, 32, n)
    amax = np.abs(w).max(1)
    byte = np.clip(np.where(amax > 0, np.frexp(amax)[1] - 1 + 127 - 7, 1), 1, 254)
    scaled = (w * np.exp2(127.0 - byte)[:, None, :]).reshape(k, n).astype(np.float32)
    words = np.ascontiguousarray(scaled.reshape(k // 512, 128, 4, n).transpose(0, 1, 3, 2)).astype(ml_dtypes.float8_e4m3fn).view(np.uint8)
    return words, np.ascontiguousarray(byte.astype(np.uint8).reshape(k // 512, 16, n))


def unpack_weight(words, scales):
    g, p, n, _ = words.shape
    vals = np.ascontiguousarray(words).view(ml_dtypes.float8_e4m3fn).astype(np.float64) * np.repeat(np.exp2(scales.astype(np.float64) - 127.0), 8, axis=1)[..., None]
    return vals.transpose(0, 1, 3, 2).reshape(g * 512, n)


def sigmoid(v):
    return 1.0 / (1.0 + np.exp(-np.maximum(v, -700.0)))


K, T, S, N, H, C = 512, 2048, 512, 512, 512, 512


def setup_inputs():
    n = np.random.standard_normal
    s = mx_kscale(K)[:, None]
    u = mx_kscale(S)
    packed_xT = pack_weight(n((K, T)) * s)
    return {
        "x_words": packed_xT[0],
        "x_scales": packed_xT[1],
        "w1": (n((K, H)) / np.sqrt(K) / s).astype(np.float32),
        "gn": (np.random.uniform(0.5, 1.5, (H, 1)) * u[:, None]).astype(np.float32),
        "w2": (n((H, N)) / np.sqrt(H) / u[:, None]).astype(np.float32),
        "gs": (np.random.uniform(0.5, 1.5, (K, 1)) / s).astype(np.float32),
        "offs": striped(np.random.permutation(T)[:S]),
        "n1": striped8(np.stack([np.random.permutation(S) for _ in range(8)])),
        "n2": striped8(np.stack([np.random.permutation(S) for _ in range(8)])),
        "n3": striped(np.random.permutation(S)),
        "n4": striped(np.random.permutation(S)),
        "cand": striped(np.random.permutation(T)[:C]),
        "n5": striped8(np.stack([np.random.permutation(S) for _ in range(8)])),
        "n6": striped8(np.stack([np.random.permutation(S) for _ in range(8)])),
        "n7": striped8(np.stack([np.random.permutation(S) for _ in range(8)])),
        "n8": striped8(np.stack([np.random.permutation(S) for _ in range(8)])),
    }


def reference(x_words, x_scales, w1, gn, w2, gs, offs, n1, n2, n3, n4, cand, n5, n6, n7, n8):
    xq = unpack_weight(x_words, x_scales)[:, unstriped(offs)]
    y = mxq(f64(w1), 0, "e4m3").T @ xq
    pa = y[np.arange(H)[:, None], runs(n1, H)]
    kr = np.exp(-0.5 * ((y - pa) ** 2))
    pb = y[np.arange(H)[:, None], runs(n2, H)]
    kr2 = np.exp(-0.5 * ((y - pb) ** 2))
    z = f64(gn) * ((kr * pa + kr2 * pb) / (kr + kr2 + 0.5))
    a = mxq(f64(w2), 0, "e4m3").T @ mxq(z, 0, "e4m3")
    x_cand = unpack_weight(x_words, x_scales)[:, unstriped(cand)]
    z2 = f64(gs) * (np.maximum(y * (sigmoid(y[:, unstriped(n3)])), y[:, unstriped(n4)]))
    b = 0.0625 * ((x_cand.T @ mxq(z2, 0, "e4m3")))
    return np.maximum(a[np.arange(N)[:, None], runs(n5, N)] + b[np.arange(C)[:, None], runs(n7, C)], a[np.arange(N)[:, None], runs(n6, N)] + b[np.arange(C)[:, None], runs(n8, C)])

@@ -1,0 +1,209 @@
+from contextlib import ExitStack
+
+import concourse.mybir as mybir
+
+K, T, S, N, H, C = 512, 2048, 512, 512, 512, 512
+FLOPS = 3 * 2 * 512 * 512 * 512
+
+F32 = mybir.dt.float32
+BF16 = mybir.dt.bfloat16
+I32 = mybir.dt.int32
+U32 = mybir.dt.uint32
+U16 = mybir.dt.uint16
+U8 = mybir.dt.uint8
+FP8X4 = mybir.dt.float8_e4m3fn_x4
+ALU = mybir.AluOpType
+ACT = mybir.ActivationFunctionType
+
+P = 128
+PACK = 4
+WINDOW = 2 * S
+LN_FLOOR = 2.0**-60
+FUSED_TERMS = 5
+
+
+def tile_picked_fkcdpathbkerngmax_none_p_kernel(
+    tc, x_words, x_scales, w1, gn, w2, gs, offs, n1, n2, n3, n4, cand, n5, n6, n7, n8, out
+):
+    nc = tc.nc
+    with ExitStack() as ctx:
+        keep = ctx.enter_context(tc.tile_pool(name="keep", bufs=1))
+        psum = ctx.enter_context(tc.psum_pool(name="psum", bufs=1))
+
+        def load_list(src, name):
+            tile = keep.tile([P, S // 16], U16, name=name)
+            nc.sync.dma_start(tile[:], src)
+            return tile
+
+        def window(name):
+            tile = keep.tile([P, WINDOW], F32, name=name)
+            nc.vector.memset(tile[:, S:WINDOW].bitcast(I32), 0)
+            return tile
+
+        xs = keep.tile([P, T], U8, name="xs")
+        for q in range(4):
+            rows = x_scales[0, 4 * q : 4 * q + 4, :].bitcast(I32)
+            nc.sync.dma_start(xs[32 * q : 32 * q + 32, :].bitcast(I32), rows.unsqueeze(0).to_broadcast([8, 4, T // 4]))
+        offs_t = load_list(offs, "offs_t")
+        xw = keep.tile([P, T], I32, name="xw")
+        nc.sync.dma_start(xw[:], x_words[0].rearrange("p n t -> p (n t)").bitcast(I32))
+        w1_rows = w1.rearrange("(p j) c -> p j c", j=PACK)
+        w1_raw = [keep.tile([P, PACK, H // 2], F32, name="w1_raw%d" % h) for h in range(2)]
+        for h in range(2):
+            nc.sync.dma_start(w1_raw[h][:], w1_rows[:, :, h * (H // 2) : (h + 1) * (H // 2)])
+        cand_t = load_list(cand, "cand_t")
+        n1_t = load_list(n1, "n1_t")
+        n2_t = load_list(n2, "n2_t")
+        w2_raw = keep.tile([P, PACK, N], F32, name="w2_raw")
+        nc.sync.dma_start(w2_raw[:], w2.rearrange("(p j) c -> p j c", j=PACK))
+        gn_t = keep.tile([P, PACK], F32, name="gn_t")
+        nc.sync.dma_start(gn_t[:], gn.rearrange("(p t) o -> p (t o)", t=PACK))
+        gs_t = keep.tile([P, PACK], F32, name="gs_t")
+        nc.sync.dma_start(gs_t[:], gs.rearrange("(p t) o -> p (t o)", t=PACK))
+        n4_t = load_list(n4, "n4_t")
+        n3_t = load_list(n3, "n3_t")
+        n5_t = load_list(n5, "n5_t")
+        n6_t = load_list(n6, "n6_t")
+        n7_t = load_list(n7, "n7_t")
+        n8_t = load_list(n8, "n8_t")
+
+        y_win = [window("y_win%d" % t) for t in range(PACK)]
+
+        tok_s = keep.tile([P, S], U8, name="tok_s", align_bytes=64)
+        nc.vector.tensor_copy(tok_s[:], xs[:].indirect(offs_t[:]))
+        tok_w = keep.tile([P, S], U32, name="tok_w", align_bytes=64)
+        nc.vector.tensor_copy(tok_w[:], xw[:].bitcast(U32).indirect(offs_t[:]))
+        cand_s = keep.tile([P, C], U8, name="cand_s", align_bytes=64)
+        nc.vector.tensor_copy(cand_s[:].rearrange("p (t m) -> p m t", t=PACK), xs[:].indirect(cand_t[:]))
+        cand_w = keep.tile([P, C], U32, name="cand_w", align_bytes=64)
+        nc.vector.tensor_copy(cand_w[:].rearrange("p (t m) -> p m t", t=PACK), xw[:].bitcast(U32).indirect(cand_t[:]))
+
+        def quantize(grouped, codes, scales, lo, hi):
+            nc.vector.quantize_mx(
+                out=codes[:, lo:hi].bitcast(FP8X4), scales=scales[:, lo:hi], in_=grouped[:, PACK * lo : PACK * hi]
+            )
+
+        def mx_tiles(name):
+            grouped = keep.tile([P, PACK * S], BF16, name=name + "_bf", align_bytes=64)
+            codes = keep.tile([P, S], U32, name=name + "_codes", align_bytes=64)
+            scales = keep.tile([P, S], U8, name=name + "_scales", align_bytes=64)
+            return grouped, codes, scales
+
+        def product(bank, lhs_w, lhs_s, rhs_w, rhs_s, t):
+            acc = psum.tile([P, S], F32, name="bank%d" % bank)
+            cols = slice(t * P, (t + 1) * P)
+            nc.tensor.matmul_mx(
+                out=acc[:], lhsT=lhs_w[:, cols].bitcast(FP8X4), lhsT_scale=lhs_s[:, cols],
+                rhs=rhs_w[:].bitcast(FP8X4), rhs_scale=rhs_s[:], start=True, stop=True,
+            )
+            return acc
+
+        w1_bf, w1_codes, w1_scales = mx_tiles("w1")
+        w1_dealt = w1_bf[:].rearrange("p (t m j) -> p m t j", t=PACK, j=PACK)
+        nc.scalar.copy(w1_dealt[:, 0 : P // 2], w1_raw[0][:].rearrange("p j (m t) -> p m t j", t=PACK))
+        nc.scalar.copy(w1_dealt[:, P // 2 : P], w1_raw[1][:].rearrange("p j (m t) -> p m t j", t=PACK))
+        for t in range(PACK):
+            quantize(w1_bf, w1_codes, w1_scales, t * P, (t + 1) * P)
+        for t in range(PACK):
+            acc = product(t, w1_codes, w1_scales, tok_w, tok_s, t)
+            nc.vector.tensor_copy(y_win[t][:, 0:S], acc[:])
+
+
+        a_win = [keep.tile([P, WINDOW], F32, name="a_win%d" % t) for t in range(PACK)]
+        picked = [tile[:].rearrange("p (a s) -> p a s", a=2) for tile in a_win]
+        kern = [keep.tile([P, 2, S], F32, name="kern%d" % t) for t in range(PACK)]
+        ksum = keep.tile([P, PACK, S], F32, name="ksum")
+        for t in range(PACK):
+            nc.scalar.activation(picked[t][:, 0, :], y_win[t][:].indirect(n1_t[:]), ACT.Copy)
+            nc.scalar.activation(picked[t][:, 1, :], y_win[t][:].indirect(n2_t[:]), ACT.Copy)
+            nc.vector.tensor_tensor(
+                kern[t][:], picked[t], y_win[t][:, 0:S].unsqueeze(1).to_broadcast([P, 2, S]), ALU.subtract
+            )
+            nc.vector.tensor_tensor(kern[t][:], kern[t][:], kern[t][:], ALU.mult)
+        for t in range(PACK):
+            nc.scalar.activation(kern[t][:], kern[t][:], ACT.Exp, scale=-0.5)
+            nc.vector.tensor_tensor(ksum[:, t, :], kern[t][:, 0, :], kern[t][:, 1, :], ALU.add)
+        w2_bf, w2_codes, w2_scales = mx_tiles("w2")
+        nc.vector.tensor_copy(
+            w2_bf[:].rearrange("p (t m j) -> p m t j", t=PACK, j=PACK),
+            w2_raw[:].rearrange("p j (m t) -> p m t j", t=PACK),
+        )
+        gn2 = keep.tile([P, PACK], F32, name="gn2")
+        nc.vector.tensor_scalar(gn2[:], gn_t[:], 2.0, None, ALU.mult)
+        quantize(w2_bf, w2_codes, w2_scales, 0, N)
+        recip = keep.tile([P, PACK, S], F32, name="recip")
+        nc.scalar.activation(recip[:], ksum[:], ACT.Ln, bias=LN_FLOOR, scale=2.0)
+        nc.scalar.activation(recip[:], recip[:], ACT.Sigmoid, scale=-1.0)
+
+        num = keep.tile([P, PACK, S], F32, name="num")
+        for t in range(PACK):
+            flat = a_win[t][:]
+            nc.vector.scalar_tensor_tensor(
+                flat, kern[t][:].rearrange("p a s -> p (a s)"), gn2[:, t : t + 1], flat, ALU.mult, ALU.mult
+            )
+        for t in range(PACK):
+            nc.vector.tensor_tensor(num[:, t, :], picked[t][:, 0, :], picked[t][:, 1, :], ALU.add)
+
+        def walk_in(planes):
+            return planes[:].rearrange("p t (c i) -> p c t i", i=4)
+
+        def walk_out(grouped):
+            return grouped[:].rearrange("p (c i t) -> p c t i", i=4, t=PACK)
+
+        z_bf, z_codes, z_scales = mx_tiles("z")
+        nc.vector.tensor_tensor(walk_out(z_bf), walk_in(num), walk_in(recip), ALU.mult)
+
+        gate = ksum
+        for t in range(PACK):
+            nc.scalar.activation(gate[:, t, :], y_win[t][:].indirect(n3_t[:]), ACT.Sigmoid)
+        for t in range(PACK):
+            nc.scalar.activation(kern[t][:, 0, :], y_win[t][:].indirect(n4_t[:]), ACT.Copy)
+        nc.vector.tensor_tensor(gate[:, 0, :], gate[:, 0, :], y_win[0][:, 0:S], ALU.mult)
+        quantize(z_bf, z_codes, z_scales, 0, S)
+        a_acc = [product(PACK + t, w2_codes, w2_scales, z_codes, z_scales, t) for t in range(PACK)]
+        for t in range(1, PACK):
+            nc.vector.tensor_tensor(gate[:, t, :], gate[:, t, :], y_win[t][:, 0:S], ALU.mult)
+        for t in range(PACK):
+            if t == 2:
+                nc.vector.tensor_copy(a_win[0][:, 0:S], a_acc[0][:])
+            nc.vector.tensor_tensor(gate[:, t, :], gate[:, t, :], kern[t][:, 0, :], ALU.max)
+        for t in range(1, PACK):
+            nc.scalar.copy(a_win[t][:, 0:S], a_acc[t][:])
+        z2_bf, z2_codes, z2_scales = mx_tiles("z2")
+        half = S // 2
+        gs_b = gs_t[:].unsqueeze(1).unsqueeze(3).to_broadcast([P, half // 4, PACK, 4])
+        for h in range(2):
+            cs = slice(h * half // 4, (h + 1) * half // 4)
+            nc.vector.tensor_tensor(walk_out(z2_bf)[:, cs], walk_in(gate)[:, cs], gs_b, ALU.mult)
+        for h in range(2):
+            quantize(z2_bf, z2_codes, z2_scales, h * half, (h + 1) * half)
+
+        a_pick = [keep.tile([P, 2, S], F32, name="a_pick%d" % t) for t in range(PACK)]
+        for t in range(PACK):
+            nc.scalar.activation(a_pick[t][:, 0, :], a_win[t][:].indirect(n5_t[:]), ACT.Copy)
+            nc.scalar.activation(a_pick[t][:, 1, :], a_win[t][:].indirect(n6_t[:]), ACT.Copy)
+        out_rows = out.rearrange("(p t) s -> p t s", t=PACK)
+        b_win = y_win
+        sums = kern
+        b_lists = (n7_t, n8_t)
+        for t in range(PACK):
+            acc = psum.tile([P, S], F32, name="bank%d" % t)
+            cols = slice(t * P, (t + 1) * P)
+            for h in range(2):
+                hs = slice(h * half, (h + 1) * half)
+                nc.tensor.matmul_mx(
+                    out=acc[:, hs], lhsT=cand_w[:, cols].bitcast(FP8X4), lhsT_scale=cand_s[:, cols],
+                    rhs=z2_codes[:, hs].bitcast(FP8X4), rhs_scale=z2_scales[:, hs], start=True, stop=True,
+                )
+            if t < 2:
+                nc.vector.tensor_scalar(b_win[t][:, 0:S], acc[:], 0.0625, None, ALU.mult)
+            else:
+                nc.scalar.activation(b_win[t][:, 0:S], acc[:], ACT.Copy, scale=0.0625)
+            for k in range(2):
+                if 2 * t + k < FUSED_TERMS:
+                    nc.vector.tensor_tensor(sums[t][:, k, :], b_win[t][:].indirect(b_lists[k][:]), a_pick[t][:, k, :], ALU.add)
+                else:
+                    nc.scalar.activation(sums[t][:, k, :], b_win[t][:].indirect(b_lists[k][:]), ACT.Copy)
+                    nc.vector.tensor_tensor(sums[t][:, k, :], sums[t][:, k, :], a_pick[t][:, k, :], ALU.add)
+            nc.vector.tensor_tensor(num[:, t, :], sums[t][:, 0, :], sums[t][:, 1, :], ALU.max)
+            nc.sync.dma_start(out_rows[:, t, :], num[:, t, :])

@@ -1,6 +1,7 @@
 from contextlib import ExitStack
 
 import concourse.mybir as mybir
+from concourse.masks import make_identity
 
 K, T, S, N, H, C = 512, 2048, 512, 512, 512, 512
 FLOPS = 3 * 2 * 512 * 512 * 512
@@ -19,7 +20,6 @@ P = 128
 PACK = 4
 WINDOW = 2 * S
 LN_FLOOR = 2.0**-60
-FUSED_TERMS = 5
 
 
 def tile_picked_fkcdpathbkerngmax_none_p_kernel(
@@ -45,13 +45,13 @@ def tile_picked_fkcdpathbkerngmax_none_p_kernel(
             rows = x_scales[0, 4 * q : 4 * q + 4, :].bitcast(I32)
             nc.sync.dma_start(xs[32 * q : 32 * q + 32, :].bitcast(I32), rows.unsqueeze(0).to_broadcast([8, 4, T // 4]))
         offs_t = load_list(offs, "offs_t")
-        xw = keep.tile([P, T], I32, name="xw")
-        nc.sync.dma_start(xw[:], x_words[0].rearrange("p n t -> p (n t)").bitcast(I32))
+        cand_t = load_list(cand, "cand_t")
         w1_rows = w1.rearrange("(p j) c -> p j c", j=PACK)
         w1_raw = [keep.tile([P, PACK, H // 2], F32, name="w1_raw%d" % h) for h in range(2)]
         for h in range(2):
             nc.sync.dma_start(w1_raw[h][:], w1_rows[:, :, h * (H // 2) : (h + 1) * (H // 2)])
-        cand_t = load_list(cand, "cand_t")
+        xw = keep.tile([P, T], I32, name="xw")
+        nc.sync.dma_start(xw[:], x_words[0].rearrange("p n t -> p (n t)").bitcast(I32))
         n1_t = load_list(n1, "n1_t")
         n2_t = load_list(n2, "n2_t")
         w2_raw = keep.tile([P, PACK, N], F32, name="w2_raw")
@@ -69,14 +69,13 @@ def tile_picked_fkcdpathbkerngmax_none_p_kernel(
 
         y_win = [window("y_win%d" % t) for t in range(PACK)]
 
+        ident = keep.tile([P, P], F32, name="ident")
+        make_identity(nc, ident[:])
+
         tok_s = keep.tile([P, S], U8, name="tok_s", align_bytes=64)
         nc.vector.tensor_copy(tok_s[:], xs[:].indirect(offs_t[:]))
-        tok_w = keep.tile([P, S], U32, name="tok_w", align_bytes=64)
-        nc.vector.tensor_copy(tok_w[:], xw[:].bitcast(U32).indirect(offs_t[:]))
         cand_s = keep.tile([P, C], U8, name="cand_s", align_bytes=64)
         nc.vector.tensor_copy(cand_s[:].rearrange("p (t m) -> p m t", t=PACK), xs[:].indirect(cand_t[:]))
-        cand_w = keep.tile([P, C], U32, name="cand_w", align_bytes=64)
-        nc.vector.tensor_copy(cand_w[:].rearrange("p (t m) -> p m t", t=PACK), xw[:].bitcast(U32).indirect(cand_t[:]))
 
         def quantize(grouped, codes, scales, lo, hi):
             nc.vector.quantize_mx(
@@ -85,7 +84,7 @@ def tile_picked_fkcdpathbkerngmax_none_p_kernel(
 
         def mx_tiles(name):
             grouped = keep.tile([P, PACK * S], BF16, name=name + "_bf", align_bytes=64)
-            codes = keep.tile([P, S], U32, name=name + "_codes", align_bytes=64)
+            codes = keep.tile([P, S], U32, name=name + "_codes", tag=name + "_codes", align_bytes=64)
             scales = keep.tile([P, S], U8, name=name + "_scales", align_bytes=64)
             return grouped, codes, scales
 
@@ -104,15 +103,21 @@ def tile_picked_fkcdpathbkerngmax_none_p_kernel(
         nc.scalar.copy(w1_dealt[:, P // 2 : P], w1_raw[1][:].rearrange("p j (m t) -> p m t j", t=PACK))
         for t in range(PACK):
             quantize(w1_bf, w1_codes, w1_scales, t * P, (t + 1) * P)
+        tok_w = keep.tile([P, S], U32, name="tok_w", align_bytes=64)
+        nc.vector.tensor_copy(tok_w[:], xw[:].bitcast(U32).indirect(offs_t[:]))
+        cand_w = keep.tile([P, C], U32, name="cand_w", align_bytes=64)
+        nc.vector.tensor_copy(cand_w[:].rearrange("p (t m) -> p m t", t=PACK), xw[:].bitcast(U32).indirect(cand_t[:]))
         for t in range(PACK):
             acc = product(t, w1_codes, w1_scales, tok_w, tok_s, t)
-            nc.vector.tensor_copy(y_win[t][:, 0:S], acc[:])
+            if t == 0:
+                nc.scalar.copy(y_win[t][:, 0:S], acc[:])
+            else:
+                nc.vector.tensor_copy(y_win[t][:, 0:S], acc[:])
 
 
         a_win = [keep.tile([P, WINDOW], F32, name="a_win%d" % t) for t in range(PACK)]
         picked = [tile[:].rearrange("p (a s) -> p a s", a=2) for tile in a_win]
         kern = [keep.tile([P, 2, S], F32, name="kern%d" % t) for t in range(PACK)]
-        ksum = keep.tile([P, PACK, S], F32, name="ksum")
         for t in range(PACK):
             nc.scalar.activation(picked[t][:, 0, :], y_win[t][:].indirect(n1_t[:]), ACT.Copy)
             nc.scalar.activation(picked[t][:, 1, :], y_win[t][:].indirect(n2_t[:]), ACT.Copy)
@@ -120,9 +125,23 @@ def tile_picked_fkcdpathbkerngmax_none_p_kernel(
                 kern[t][:], picked[t], y_win[t][:, 0:S].unsqueeze(1).to_broadcast([P, 2, S]), ALU.subtract
             )
             nc.vector.tensor_tensor(kern[t][:], kern[t][:], kern[t][:], ALU.mult)
+
+        def add_turned(banks, pair, t):
+            for b in range(PACK):
+                for k in range(2):
+                    nc.tensor.matmul(
+                        banks[b][:, t, :], lhsT=pair[:, k, b * P : (b + 1) * P], rhs=ident[:],
+                        is_transpose=True, start=(k == 0), stop=(k == 1),
+                    )
+
+        def paired(bank):
+            return bank[:].rearrange("j (u e) p -> j u p e", e=2)
+
+        ksum = [psum.tile([P, PACK, P], F32, name="bank%d" % (PACK + b)) for b in range(PACK)]
         for t in range(PACK):
             nc.scalar.activation(kern[t][:], kern[t][:], ACT.Exp, scale=-0.5)
-            nc.vector.tensor_tensor(ksum[:, t, :], kern[t][:, 0, :], kern[t][:, 1, :], ALU.add)
+            add_turned(ksum, kern[t], t)
+
         w2_bf, w2_codes, w2_scales = mx_tiles("w2")
         nc.vector.tensor_copy(
             w2_bf[:].rearrange("p (t m j) -> p m t j", t=PACK, j=PACK),
@@ -131,18 +150,23 @@ def tile_picked_fkcdpathbkerngmax_none_p_kernel(
         gn2 = keep.tile([P, PACK], F32, name="gn2")
         nc.vector.tensor_scalar(gn2[:], gn_t[:], 2.0, None, ALU.mult)
         quantize(w2_bf, w2_codes, w2_scales, 0, N)
-        recip = keep.tile([P, PACK, S], F32, name="recip")
-        nc.scalar.activation(recip[:], ksum[:], ACT.Ln, bias=LN_FLOOR, scale=2.0)
-        nc.scalar.activation(recip[:], recip[:], ACT.Sigmoid, scale=-1.0)
 
-        num = keep.tile([P, PACK, S], F32, name="num")
+        logs = keep.tile([P, PACK, S], F32, name="logs")
+        recip = keep.tile([P, PACK, S], F32, name="recip")
+        for b in range(PACK):
+            nc.scalar.activation(
+                logs[:, b, :].rearrange("j (u p e) -> j u p e", u=2, e=2), paired(ksum[b]), ACT.Ln, bias=LN_FLOOR, scale=2.0
+            )
+        for b in range(PACK):
+            nc.scalar.activation(recip[:, b, :], logs[:, b, :], ACT.Sigmoid, scale=-1.0)
+
+        numer = [psum.tile([P, PACK, P], F32, name="bank%d" % b) for b in range(PACK)]
         for t in range(PACK):
             flat = a_win[t][:]
             nc.vector.scalar_tensor_tensor(
                 flat, kern[t][:].rearrange("p a s -> p (a s)"), gn2[:, t : t + 1], flat, ALU.mult, ALU.mult
             )
-        for t in range(PACK):
-            nc.vector.tensor_tensor(num[:, t, :], picked[t][:, 0, :], picked[t][:, 1, :], ALU.add)
+            add_turned(numer, picked[t], t)
 
         def walk_in(planes):
             return planes[:].rearrange("p t (c i) -> p c t i", i=4)
@@ -151,23 +175,37 @@ def tile_picked_fkcdpathbkerngmax_none_p_kernel(
             return grouped[:].rearrange("p (c i t) -> p c t i", i=4, t=PACK)
 
         z_bf, z_codes, z_scales = mx_tiles("z")
-        nc.vector.tensor_tensor(walk_out(z_bf), walk_in(num), walk_in(recip), ALU.mult)
+        z_turned = keep.tile([P, PACK, H], BF16, name="z_turned")
+        z_back = [psum.tile([P, 2, 2, P], F32, name="bank%d" % (PACK + g)) for g in range(2)]
+        nc.vector.tensor_copy(kern[0][:, 0, :], y_win[0][:].indirect(n4_t[:]))
+        for b in range(PACK):
+            nc.vector.tensor_tensor(
+                z_turned[:, b, :].rearrange("j (u p e) -> j u p e", u=2, e=2),
+                paired(numer[b]),
+                recip[:, b, :].rearrange("j (u p e) -> j u p e", u=2, e=2),
+                ALU.mult,
+            )
+            words = z_turned[:, b, :].bitcast(F32)
+            for u in range(2):
+                nc.tensor.transpose(z_back[b // 2][:, b % 2, u, :], words[:, u * P : (u + 1) * P], ident[:])
+        nc.vector.tensor_copy(kern[1][:, 0, :], y_win[1][:].indirect(n4_t[:]))
+        z_words = z_bf[:].bitcast(F32).rearrange("p (g b j u) -> p g b j u", g=2, b=2, u=2)
+        for g in range(2):
+            nc.vector.tensor_copy(z_words[:, g], z_back[g][:].rearrange("p b u j -> p b j u"))
 
-        gate = ksum
+        gate = logs
         for t in range(PACK):
             nc.scalar.activation(gate[:, t, :], y_win[t][:].indirect(n3_t[:]), ACT.Sigmoid)
-        for t in range(PACK):
+        for t in range(2, PACK):
             nc.scalar.activation(kern[t][:, 0, :], y_win[t][:].indirect(n4_t[:]), ACT.Copy)
         nc.vector.tensor_tensor(gate[:, 0, :], gate[:, 0, :], y_win[0][:, 0:S], ALU.mult)
         quantize(z_bf, z_codes, z_scales, 0, S)
-        a_acc = [product(PACK + t, w2_codes, w2_scales, z_codes, z_scales, t) for t in range(PACK)]
+        a_acc = [product(t, w2_codes, w2_scales, z_codes, z_scales, t) for t in range(PACK)]
         for t in range(1, PACK):
             nc.vector.tensor_tensor(gate[:, t, :], gate[:, t, :], y_win[t][:, 0:S], ALU.mult)
         for t in range(PACK):
-            if t == 2:
-                nc.vector.tensor_copy(a_win[0][:, 0:S], a_acc[0][:])
             nc.vector.tensor_tensor(gate[:, t, :], gate[:, t, :], kern[t][:, 0, :], ALU.max)
-        for t in range(1, PACK):
+        for t in range(PACK):
             nc.scalar.copy(a_win[t][:, 0:S], a_acc[t][:])
         z2_bf, z2_codes, z2_scales = mx_tiles("z2")
         half = S // 2
@@ -178,16 +216,16 @@ def tile_picked_fkcdpathbkerngmax_none_p_kernel(
         for h in range(2):
             quantize(z2_bf, z2_codes, z2_scales, h * half, (h + 1) * half)
 
-        a_pick = [keep.tile([P, 2, S], F32, name="a_pick%d" % t) for t in range(PACK)]
-        for t in range(PACK):
-            nc.scalar.activation(a_pick[t][:, 0, :], a_win[t][:].indirect(n5_t[:]), ACT.Copy)
-            nc.scalar.activation(a_pick[t][:, 1, :], a_win[t][:].indirect(n6_t[:]), ACT.Copy)
-        out_rows = out.rearrange("(p t) s -> p t s", t=PACK)
+        def pick_a(dst, t):
+            nc.scalar.activation(dst[:, 0, :], a_win[t][:].indirect(n5_t[:]), ACT.Copy)
+            nc.scalar.activation(dst[:, 1, :], a_win[t][:].indirect(n6_t[:]), ACT.Copy)
+
+        a_early = keep.tile([P, 2, 2, S], F32, name="a_early")
+        for t in range(2):
+            pick_a(a_early[:, t], t)
         b_win = y_win
-        sums = kern
-        b_lists = (n7_t, n8_t)
         for t in range(PACK):
-            acc = psum.tile([P, S], F32, name="bank%d" % t)
+            acc = psum.tile([P, S], F32, name="bank%d" % (PACK + t))
             cols = slice(t * P, (t + 1) * P)
             for h in range(2):
                 hs = slice(h * half, (h + 1) * half)
@@ -195,15 +233,32 @@ def tile_picked_fkcdpathbkerngmax_none_p_kernel(
                     out=acc[:, hs], lhsT=cand_w[:, cols].bitcast(FP8X4), lhsT_scale=cand_s[:, cols],
                     rhs=z2_codes[:, hs].bitcast(FP8X4), rhs_scale=z2_scales[:, hs], start=True, stop=True,
                 )
-            if t < 2:
+            if t == 0:
                 nc.vector.tensor_scalar(b_win[t][:, 0:S], acc[:], 0.0625, None, ALU.mult)
             else:
                 nc.scalar.activation(b_win[t][:, 0:S], acc[:], ACT.Copy, scale=0.0625)
+        a_late = keep.tile([P, 2, 2, S], F32, name="a_late", tag="z2_codes", align_bytes=64)
+        for t in range(2):
+            pick_a(a_late[:, t], 2 + t)
+        a_pick = [a_early[:, 0], a_early[:, 1], a_late[:, 0], a_late[:, 1]]
+
+        out_rows = out.rearrange("(p t) s -> p t s", t=PACK)
+        sums = kern
+        best = recip
+        b_lists = (n7_t, n8_t)
+        last = PACK - 1
+        for t in range(last):
             for k in range(2):
-                if 2 * t + k < FUSED_TERMS:
-                    nc.vector.tensor_tensor(sums[t][:, k, :], b_win[t][:].indirect(b_lists[k][:]), a_pick[t][:, k, :], ALU.add)
-                else:
-                    nc.scalar.activation(sums[t][:, k, :], b_win[t][:].indirect(b_lists[k][:]), ACT.Copy)
-                    nc.vector.tensor_tensor(sums[t][:, k, :], sums[t][:, k, :], a_pick[t][:, k, :], ALU.add)
-            nc.vector.tensor_tensor(num[:, t, :], sums[t][:, 0, :], sums[t][:, 1, :], ALU.max)
-            nc.sync.dma_start(out_rows[:, t, :], num[:, t, :])
+                nc.vector.tensor_tensor(sums[t][:, k, :], b_win[t][:].indirect(b_lists[k][:]), a_pick[t][:, k, :], ALU.add)
+            nc.vector.tensor_tensor(best[:, t, :], sums[t][:, 0, :], sums[t][:, 1, :], ALU.max)
+            nc.sync.dma_start(out_rows[:, t, :], best[:, t, :])
+        nc.scalar.activation(sums[last][:, 0, :], b_win[last][:].indirect(n7_t[:]), ACT.Copy)
+        nc.vector.tensor_tensor(sums[last][:, 0, :], sums[last][:, 0, :], a_pick[last][:, 0, :], ALU.add)
+        for h in range(2):
+            hs = slice(h * half, (h + 1) * half)
+            nc.scalar.activation(
+                sums[last][:, 1, hs], b_win[last][:].indirect(n8_t[:, h * half // 16 : (h + 1) * half // 16]), ACT.Copy
+            )
+            nc.vector.tensor_tensor(sums[last][:, 1, hs], sums[last][:, 1, hs], a_pick[last][:, 1, hs], ALU.add)
+            nc.vector.tensor_tensor(best[:, last, hs], sums[last][:, 0, hs], sums[last][:, 1, hs], ALU.max)
+            nc.sync.dma_start(out_rows[:, last, hs], best[:, last, hs])

@@ -54,13 +54,13 @@ def tile_picked_fkcdpathbkerngmax_none_p_kernel(
         nc.sync.dma_start(xw[:], x_words[0].rearrange("p n t -> p (n t)").bitcast(I32))
         n1_t = load_list(n1, "n1_t")
         n2_t = load_list(n2, "n2_t")
+        n4_t = load_list(n4, "n4_t")
         w2_raw = keep.tile([P, PACK, N], F32, name="w2_raw")
         nc.sync.dma_start(w2_raw[:], w2.rearrange("(p j) c -> p j c", j=PACK))
         gn_t = keep.tile([P, PACK], F32, name="gn_t")
         nc.sync.dma_start(gn_t[:], gn.rearrange("(p t) o -> p (t o)", t=PACK))
         gs_t = keep.tile([P, PACK], F32, name="gs_t")
         nc.sync.dma_start(gs_t[:], gs.rearrange("(p t) o -> p (t o)", t=PACK))
-        n4_t = load_list(n4, "n4_t")
         n3_t = load_list(n3, "n3_t")
         n5_t = load_list(n5, "n5_t")
         n6_t = load_list(n6, "n6_t")
@@ -83,7 +83,7 @@ def tile_picked_fkcdpathbkerngmax_none_p_kernel(
             )
 
         def mx_tiles(name):
-            grouped = keep.tile([P, PACK * S], BF16, name=name + "_bf", align_bytes=64)
+            grouped = keep.tile([P, PACK * S], BF16, name=name + "_bf", tag=name + "_bf", align_bytes=64)
             codes = keep.tile([P, S], U32, name=name + "_codes", tag=name + "_codes", align_bytes=64)
             scales = keep.tile([P, S], U8, name=name + "_scales", align_bytes=64)
             return grouped, codes, scales
@@ -107,8 +107,10 @@ def tile_picked_fkcdpathbkerngmax_none_p_kernel(
         nc.vector.tensor_copy(tok_w[:], xw[:].bitcast(U32).indirect(offs_t[:]))
         cand_w = keep.tile([P, C], U32, name="cand_w", align_bytes=64)
         nc.vector.tensor_copy(cand_w[:].rearrange("p (t m) -> p m t", t=PACK), xw[:].bitcast(U32).indirect(cand_t[:]))
+        y_acc = []
         for t in range(PACK):
             acc = product(t, w1_codes, w1_scales, tok_w, tok_s, t)
+            y_acc.append(acc)
             if t == 0:
                 nc.scalar.copy(y_win[t][:, 0:S], acc[:])
             else:
@@ -117,14 +119,18 @@ def tile_picked_fkcdpathbkerngmax_none_p_kernel(
 
         a_win = [keep.tile([P, WINDOW], F32, name="a_win%d" % t) for t in range(PACK)]
         picked = [tile[:].rearrange("p (a s) -> p a s", a=2) for tile in a_win]
+        other = keep.tile([P, PACK, S], F32, name="other")
         kern = [keep.tile([P, 2, S], F32, name="kern%d" % t) for t in range(PACK)]
         for t in range(PACK):
             nc.scalar.activation(picked[t][:, 0, :], y_win[t][:].indirect(n1_t[:]), ACT.Copy)
             nc.scalar.activation(picked[t][:, 1, :], y_win[t][:].indirect(n2_t[:]), ACT.Copy)
+            diff = kern[t] if t < PACK - 1 else keep.tile([P, 2, S], F32, name="diff", tag="w2_bf", align_bytes=64)
             nc.vector.tensor_tensor(
-                kern[t][:], picked[t], y_win[t][:, 0:S].unsqueeze(1).to_broadcast([P, 2, S]), ALU.subtract
+                diff[:], picked[t], y_acc[t][:].unsqueeze(1).to_broadcast([P, 2, S]), ALU.subtract
             )
-            nc.vector.tensor_tensor(kern[t][:], kern[t][:], kern[t][:], ALU.mult)
+            squarer = nc.gpsimd if t < PACK - 1 else nc.vector
+            squarer.tensor_tensor(kern[t][:], diff[:], diff[:], ALU.mult)
+            nc.vector.tensor_copy(other[:, t, :], y_win[t][:].indirect(n4_t[:]))
 
         def add_turned(banks, pair, t):
             for b in range(PACK):
@@ -177,7 +183,6 @@ def tile_picked_fkcdpathbkerngmax_none_p_kernel(
         z_bf, z_codes, z_scales = mx_tiles("z")
         z_turned = keep.tile([P, PACK, H], BF16, name="z_turned")
         z_back = [psum.tile([P, 2, 2, P], F32, name="bank%d" % (PACK + g)) for g in range(2)]
-        nc.vector.tensor_copy(kern[0][:, 0, :], y_win[0][:].indirect(n4_t[:]))
         for b in range(PACK):
             nc.vector.tensor_tensor(
                 z_turned[:, b, :].rearrange("j (u p e) -> j u p e", u=2, e=2),
@@ -188,7 +193,6 @@ def tile_picked_fkcdpathbkerngmax_none_p_kernel(
             words = z_turned[:, b, :].bitcast(F32)
             for u in range(2):
                 nc.tensor.transpose(z_back[b // 2][:, b % 2, u, :], words[:, u * P : (u + 1) * P], ident[:])
-        nc.vector.tensor_copy(kern[1][:, 0, :], y_win[1][:].indirect(n4_t[:]))
         z_words = z_bf[:].bitcast(F32).rearrange("p (g b j u) -> p g b j u", g=2, b=2, u=2)
         for g in range(2):
             nc.vector.tensor_copy(z_words[:, g], z_back[g][:].rearrange("p b u j -> p b j u"))
@@ -196,15 +200,13 @@ def tile_picked_fkcdpathbkerngmax_none_p_kernel(
         gate = logs
         for t in range(PACK):
             nc.scalar.activation(gate[:, t, :], y_win[t][:].indirect(n3_t[:]), ACT.Sigmoid)
-        for t in range(2, PACK):
-            nc.scalar.activation(kern[t][:, 0, :], y_win[t][:].indirect(n4_t[:]), ACT.Copy)
         nc.vector.tensor_tensor(gate[:, 0, :], gate[:, 0, :], y_win[0][:, 0:S], ALU.mult)
         quantize(z_bf, z_codes, z_scales, 0, S)
         a_acc = [product(t, w2_codes, w2_scales, z_codes, z_scales, t) for t in range(PACK)]
         for t in range(1, PACK):
             nc.vector.tensor_tensor(gate[:, t, :], gate[:, t, :], y_win[t][:, 0:S], ALU.mult)
-        for t in range(PACK):
-            nc.vector.tensor_tensor(gate[:, t, :], gate[:, t, :], kern[t][:, 0, :], ALU.max)
+            nc.vector.tensor_tensor(gate[:, t - 1, :], gate[:, t - 1, :], other[:, t - 1, :], ALU.max)
+        nc.vector.tensor_tensor(gate[:, PACK - 1, :], gate[:, PACK - 1, :], other[:, PACK - 1, :], ALU.max)
         for t in range(PACK):
             nc.scalar.copy(a_win[t][:, 0:S], a_acc[t][:])
         z2_bf, z2_codes, z2_scales = mx_tiles("z2")

from contextlib import ExitStack

import concourse.mybir as mybir
from concourse.masks import make_identity

K, T, S, N, H, C = 512, 2048, 512, 512, 512, 512
FLOPS = 3 * 2 * 512 * 512 * 512

F32 = mybir.dt.float32
BF16 = mybir.dt.bfloat16
I32 = mybir.dt.int32
U32 = mybir.dt.uint32
U16 = mybir.dt.uint16
U8 = mybir.dt.uint8
FP8X4 = mybir.dt.float8_e4m3fn_x4
ALU = mybir.AluOpType
ACT = mybir.ActivationFunctionType

P = 128
PACK = 4
WINDOW = 2 * S
LN_FLOOR = 2.0**-60


def tile_picked_fkcdpathbkerngmax_none_p_kernel(
    tc, x_words, x_scales, w1, gn, w2, gs, offs, n1, n2, n3, n4, cand, n5, n6, n7, n8, out
):
    nc = tc.nc
    with ExitStack() as ctx:
        keep = ctx.enter_context(tc.tile_pool(name="keep", bufs=1))
        psum = ctx.enter_context(tc.psum_pool(name="psum", bufs=1))

        def load_list(src, name):
            tile = keep.tile([P, S // 16], U16, name=name)
            nc.sync.dma_start(tile[:], src)
            return tile

        def window(name):
            tile = keep.tile([P, WINDOW], F32, name=name)
            nc.vector.memset(tile[:, S:WINDOW].bitcast(I32), 0)
            return tile

        xs = keep.tile([P, T], U8, name="xs")
        for q in range(4):
            rows = x_scales[0, 4 * q : 4 * q + 4, :].bitcast(I32)
            nc.sync.dma_start(xs[32 * q : 32 * q + 32, :].bitcast(I32), rows.unsqueeze(0).to_broadcast([8, 4, T // 4]))
        offs_t = load_list(offs, "offs_t")
        cand_t = load_list(cand, "cand_t")
        w1_rows = w1.rearrange("(p j) c -> p j c", j=PACK)
        w1_raw = [keep.tile([P, PACK, H // 2], F32, name="w1_raw%d" % h) for h in range(2)]
        for h in range(2):
            nc.sync.dma_start(w1_raw[h][:], w1_rows[:, :, h * (H // 2) : (h + 1) * (H // 2)])
        xw = keep.tile([P, T], I32, name="xw")
        nc.sync.dma_start(xw[:], x_words[0].rearrange("p n t -> p (n t)").bitcast(I32))
        n1_t = load_list(n1, "n1_t")
        n2_t = load_list(n2, "n2_t")
        n4_t = load_list(n4, "n4_t")
        w2_raw = keep.tile([P, PACK, N], F32, name="w2_raw")
        nc.sync.dma_start(w2_raw[:], w2.rearrange("(p j) c -> p j c", j=PACK))
        gn_t = keep.tile([P, PACK], F32, name="gn_t")
        nc.sync.dma_start(gn_t[:], gn.rearrange("(p t) o -> p (t o)", t=PACK))
        gs_t = keep.tile([P, PACK], F32, name="gs_t")
        nc.sync.dma_start(gs_t[:], gs.rearrange("(p t) o -> p (t o)", t=PACK))
        n3_t = load_list(n3, "n3_t")
        n5_t = load_list(n5, "n5_t")
        n6_t = load_list(n6, "n6_t")
        n7_t = load_list(n7, "n7_t")
        n8_t = load_list(n8, "n8_t")

        y_win = [window("y_win%d" % t) for t in range(PACK)]

        ident = keep.tile([P, P], F32, name="ident")
        make_identity(nc, ident[:])

        tok_s = keep.tile([P, S], U8, name="tok_s", align_bytes=64)
        nc.vector.tensor_copy(tok_s[:], xs[:].indirect(offs_t[:]))
        cand_s = keep.tile([P, C], U8, name="cand_s", align_bytes=64)
        nc.vector.tensor_copy(cand_s[:].rearrange("p (t m) -> p m t", t=PACK), xs[:].indirect(cand_t[:]))

        def quantize(grouped, codes, scales, lo, hi):
            nc.vector.quantize_mx(
                out=codes[:, lo:hi].bitcast(FP8X4), scales=scales[:, lo:hi], in_=grouped[:, PACK * lo : PACK * hi]
            )

        def mx_tiles(name):
            grouped = keep.tile([P, PACK * S], BF16, name=name + "_bf", tag=name + "_bf", align_bytes=64)
            codes = keep.tile([P, S], U32, name=name + "_codes", tag=name + "_codes", align_bytes=64)
            scales = keep.tile([P, S], U8, name=name + "_scales", align_bytes=64)
            return grouped, codes, scales

        def product(bank, lhs_w, lhs_s, rhs_w, rhs_s, t):
            acc = psum.tile([P, S], F32, name="bank%d" % bank)
            cols = slice(t * P, (t + 1) * P)
            nc.tensor.matmul_mx(
                out=acc[:], lhsT=lhs_w[:, cols].bitcast(FP8X4), lhsT_scale=lhs_s[:, cols],
                rhs=rhs_w[:].bitcast(FP8X4), rhs_scale=rhs_s[:], start=True, stop=True,
            )
            return acc

        w1_bf, w1_codes, w1_scales = mx_tiles("w1")
        w1_dealt = w1_bf[:].rearrange("p (t m j) -> p m t j", t=PACK, j=PACK)
        nc.scalar.copy(w1_dealt[:, 0 : P // 2], w1_raw[0][:].rearrange("p j (m t) -> p m t j", t=PACK))
        nc.scalar.copy(w1_dealt[:, P // 2 : P], w1_raw[1][:].rearrange("p j (m t) -> p m t j", t=PACK))
        for t in range(PACK):
            quantize(w1_bf, w1_codes, w1_scales, t * P, (t + 1) * P)
        tok_w = keep.tile([P, S], U32, name="tok_w", align_bytes=64)
        nc.vector.tensor_copy(tok_w[:], xw[:].bitcast(U32).indirect(offs_t[:]))
        cand_w = keep.tile([P, C], U32, name="cand_w", align_bytes=64)
        nc.vector.tensor_copy(cand_w[:].rearrange("p (t m) -> p m t", t=PACK), xw[:].bitcast(U32).indirect(cand_t[:]))
        y_acc = []
        for t in range(PACK):
            acc = product(t, w1_codes, w1_scales, tok_w, tok_s, t)
            y_acc.append(acc)
            if t == 0:
                nc.scalar.copy(y_win[t][:, 0:S], acc[:])
            else:
                nc.vector.tensor_copy(y_win[t][:, 0:S], acc[:])


        a_win = [keep.tile([P, WINDOW], F32, name="a_win%d" % t) for t in range(PACK)]
        picked = [tile[:].rearrange("p (a s) -> p a s", a=2) for tile in a_win]
        other = keep.tile([P, PACK, S], F32, name="other")
        kern = [keep.tile([P, 2, S], F32, name="kern%d" % t) for t in range(PACK)]
        for t in range(PACK):
            nc.scalar.activation(picked[t][:, 0, :], y_win[t][:].indirect(n1_t[:]), ACT.Copy)
            nc.scalar.activation(picked[t][:, 1, :], y_win[t][:].indirect(n2_t[:]), ACT.Copy)
            diff = kern[t] if t < PACK - 1 else keep.tile([P, 2, S], F32, name="diff", tag="w2_bf", align_bytes=64)
            nc.vector.tensor_tensor(
                diff[:], picked[t], y_acc[t][:].unsqueeze(1).to_broadcast([P, 2, S]), ALU.subtract
            )
            squarer = nc.gpsimd if t < PACK - 1 else nc.vector
            squarer.tensor_tensor(kern[t][:], diff[:], diff[:], ALU.mult)
            nc.vector.tensor_copy(other[:, t, :], y_win[t][:].indirect(n4_t[:]))

        def add_turned(banks, pair, t):
            for b in range(PACK):
                for k in range(2):
                    nc.tensor.matmul(
                        banks[b][:, t, :], lhsT=pair[:, k, b * P : (b + 1) * P], rhs=ident[:],
                        is_transpose=True, start=(k == 0), stop=(k == 1),
                    )

        def paired(bank):
            return bank[:].rearrange("j (u e) p -> j u p e", e=2)

        ksum = [psum.tile([P, PACK, P], F32, name="bank%d" % (PACK + b)) for b in range(PACK)]
        for t in range(PACK):
            nc.scalar.activation(kern[t][:], kern[t][:], ACT.Exp, scale=-0.5)
            add_turned(ksum, kern[t], t)

        w2_bf, w2_codes, w2_scales = mx_tiles("w2")
        nc.vector.tensor_copy(
            w2_bf[:].rearrange("p (t m j) -> p m t j", t=PACK, j=PACK),
            w2_raw[:].rearrange("p j (m t) -> p m t j", t=PACK),
        )
        gn2 = keep.tile([P, PACK], F32, name="gn2")
        nc.vector.tensor_scalar(gn2[:], gn_t[:], 2.0, None, ALU.mult)
        quantize(w2_bf, w2_codes, w2_scales, 0, N)

        logs = keep.tile([P, PACK, S], F32, name="logs")
        recip = keep.tile([P, PACK, S], F32, name="recip")
        for b in range(PACK):
            nc.scalar.activation(
                logs[:, b, :].rearrange("j (u p e) -> j u p e", u=2, e=2), paired(ksum[b]), ACT.Ln, bias=LN_FLOOR, scale=2.0
            )
        for b in range(PACK):
            nc.scalar.activation(recip[:, b, :], logs[:, b, :], ACT.Sigmoid, scale=-1.0)

        numer = [psum.tile([P, PACK, P], F32, name="bank%d" % b) for b in range(PACK)]
        for t in range(PACK):
            flat = a_win[t][:]
            nc.vector.scalar_tensor_tensor(
                flat, kern[t][:].rearrange("p a s -> p (a s)"), gn2[:, t : t + 1], flat, ALU.mult, ALU.mult
            )
            add_turned(numer, picked[t], t)

        def walk_in(planes):
            return planes[:].rearrange("p t (c i) -> p c t i", i=4)

        def walk_out(grouped):
            return grouped[:].rearrange("p (c i t) -> p c t i", i=4, t=PACK)

        z_bf, z_codes, z_scales = mx_tiles("z")
        z_turned = keep.tile([P, PACK, H], BF16, name="z_turned")
        z_back = [psum.tile([P, 2, 2, P], F32, name="bank%d" % (PACK + g)) for g in range(2)]
        for b in range(PACK):
            nc.vector.tensor_tensor(
                z_turned[:, b, :].rearrange("j (u p e) -> j u p e", u=2, e=2),
                paired(numer[b]),
                recip[:, b, :].rearrange("j (u p e) -> j u p e", u=2, e=2),
                ALU.mult,
            )
            words = z_turned[:, b, :].bitcast(F32)
            for u in range(2):
                nc.tensor.transpose(z_back[b // 2][:, b % 2, u, :], words[:, u * P : (u + 1) * P], ident[:])
        z_words = z_bf[:].bitcast(F32).rearrange("p (g b j u) -> p g b j u", g=2, b=2, u=2)
        for g in range(2):
            nc.vector.tensor_copy(z_words[:, g], z_back[g][:].rearrange("p b u j -> p b j u"))

        gate = logs
        for t in range(PACK):
            nc.scalar.activation(gate[:, t, :], y_win[t][:].indirect(n3_t[:]), ACT.Sigmoid)
        nc.vector.tensor_tensor(gate[:, 0, :], gate[:, 0, :], y_win[0][:, 0:S], ALU.mult)
        quantize(z_bf, z_codes, z_scales, 0, S)
        a_acc = [product(t, w2_codes, w2_scales, z_codes, z_scales, t) for t in range(PACK)]
        for t in range(1, PACK):
            nc.vector.tensor_tensor(gate[:, t, :], gate[:, t, :], y_win[t][:, 0:S], ALU.mult)
            nc.vector.tensor_tensor(gate[:, t - 1, :], gate[:, t - 1, :], other[:, t - 1, :], ALU.max)
        nc.vector.tensor_tensor(gate[:, PACK - 1, :], gate[:, PACK - 1, :], other[:, PACK - 1, :], ALU.max)
        for t in range(PACK):
            nc.scalar.copy(a_win[t][:, 0:S], a_acc[t][:])
        z2_bf, z2_codes, z2_scales = mx_tiles("z2")
        half = S // 2
        gs_b = gs_t[:].unsqueeze(1).unsqueeze(3).to_broadcast([P, half // 4, PACK, 4])
        for h in range(2):
            cs = slice(h * half // 4, (h + 1) * half // 4)
            nc.vector.tensor_tensor(walk_out(z2_bf)[:, cs], walk_in(gate)[:, cs], gs_b, ALU.mult)
        for h in range(2):
            quantize(z2_bf, z2_codes, z2_scales, h * half, (h + 1) * half)

        def pick_a(dst, t):
            nc.scalar.activation(dst[:, 0, :], a_win[t][:].indirect(n5_t[:]), ACT.Copy)
            nc.scalar.activation(dst[:, 1, :], a_win[t][:].indirect(n6_t[:]), ACT.Copy)

        a_early = keep.tile([P, 2, 2, S], F32, name="a_early")
        for t in range(2):
            pick_a(a_early[:, t], t)
        b_win = y_win
        for t in range(PACK):
            acc = psum.tile([P, S], F32, name="bank%d" % (PACK + t))
            cols = slice(t * P, (t + 1) * P)
            for h in range(2):
                hs = slice(h * half, (h + 1) * half)
                nc.tensor.matmul_mx(
                    out=acc[:, hs], lhsT=cand_w[:, cols].bitcast(FP8X4), lhsT_scale=cand_s[:, cols],
                    rhs=z2_codes[:, hs].bitcast(FP8X4), rhs_scale=z2_scales[:, hs], start=True, stop=True,
                )
            if t == 0:
                nc.vector.tensor_scalar(b_win[t][:, 0:S], acc[:], 0.0625, None, ALU.mult)
            else:
                nc.scalar.activation(b_win[t][:, 0:S], acc[:], ACT.Copy, scale=0.0625)
        a_late = keep.tile([P, 2, 2, S], F32, name="a_late", tag="z2_codes", align_bytes=64)
        for t in range(2):
            pick_a(a_late[:, t], 2 + t)
        a_pick = [a_early[:, 0], a_early[:, 1], a_late[:, 0], a_late[:, 1]]

        out_rows = out.rearrange("(p t) s -> p t s", t=PACK)
        sums = kern
        best = recip
        b_lists = (n7_t, n8_t)
        last = PACK - 1
        for t in range(last):
            for k in range(2):
                nc.vector.tensor_tensor(sums[t][:, k, :], b_win[t][:].indirect(b_lists[k][:]), a_pick[t][:, k, :], ALU.add)
            nc.vector.tensor_tensor(best[:, t, :], sums[t][:, 0, :], sums[t][:, 1, :], ALU.max)
            nc.sync.dma_start(out_rows[:, t, :], best[:, t, :])
        nc.scalar.activation(sums[last][:, 0, :], b_win[last][:].indirect(n7_t[:]), ACT.Copy)
        nc.vector.tensor_tensor(sums[last][:, 0, :], sums[last][:, 0, :], a_pick[last][:, 0, :], ALU.add)
        for h in range(2):
            hs = slice(h * half, (h + 1) * half)
            nc.scalar.activation(
                sums[last][:, 1, hs], b_win[last][:].indirect(n8_t[:, h * half // 16 : (h + 1) * half // 16]), ACT.Copy
            )
            nc.vector.tensor_tensor(sums[last][:, 1, hs], sums[last][:, 1, hs], a_pick[last][:, 1, hs], ALU.add)
            nc.vector.tensor_tensor(best[:, last, hs], sums[last][:, 0, hs], sums[last][:, 1, hs], ALU.max)
            nc.sync.dma_start(out_rows[:, last, hs], best[:, last, hs])
